import numpy as np
import ml_dtypes

BF16 = ml_dtypes.bfloat16


def bf(x):
    return np.asarray(x, np.float32).astype(BF16)


def f32(x):
    return np.asarray(x, np.float32)


def f64(x):
    return np.asarray(x).astype(np.float64)


def striped(idx):
    return np.concatenate([l.reshape(-1, 16).T for l in idx])


def rows(idx, k):
    return np.tile(np.repeat(idx, 16, axis=0), (k // (16 * 8), 1))


def look(tab, idx):
    return np.take_along_axis(f64(tab), rows(idx, len(tab)), axis=1)


K, S, H, D, V, N = 128, 2048, 256, 2, 512, 1024


def setup_inputs():
    return {"z": bf(np.random.standard_normal((H, S))), "wt": bf(np.random.standard_normal((H, K)) / np.sqrt(H)), "u0": f32(np.random.uniform(0.2, 1.0, (K, V))), "u1": f32(np.random.uniform(0.2, 1.0, (K, V))), "offs": striped(np.stack([np.random.permutation(S)[:N] for _ in range(8)]))}


def reference(z, wt, u0, u1, offs):
    idx = np.stack([g.T.reshape(-1) for g in np.split(offs, 8)])
    tab = f64(wt).T @ f64(z)
    x = f64(u0) * look(tab, idx[:, :V]) + f64(u1) * look(tab, idx[:, 1 * V:2 * V])
    return x

@@ -1,0 +1,68 @@
+import concourse.mybir as mybir
+
+P = 128
+H = 256
+S = 2048
+V = 512
+LOOKUPS = 2
+GROUP = 16
+BANKS = 8
+STRIP = S // BANKS
+LOAD_COLS = 1024
+OUT_PIECES = 2
+FLOPS = 2 * H * P * S
+
+BF16, F32, U16 = mybir.dt.bfloat16, mybir.dt.float32, mybir.dt.uint16
+MULT, ADD = mybir.AluOpType.mult, mybir.AluOpType.add
+
+
+def tile_lookup_pjmix_out_kernel(tc, z, wt, u0, u1, offs, out):
+    nc = tc.nc
+    passes = H // P
+    with (
+        tc.tile_pool(name="held", bufs=1) as held,
+        tc.psum_pool(name="psum", bufs=1) as psum,
+    ):
+        wt_sb = held.tile([P, passes * P], BF16, name="wt_sb")
+        nc.sync.dma_start(wt_sb[:], wt.rearrange("(p c) r -> p (c r)", c=passes))
+        z_by_pass = z.rearrange("(p c) s -> c p s", c=passes)
+        z_sb = {}
+        for part in range(S // LOAD_COLS):
+            for c in range(passes):
+                z_sb[part, c] = held.tile([P, LOAD_COLS], BF16, name=f"z_{part}_{c}")
+                nc.sync.dma_start(z_sb[part, c][:], z_by_pass[c, :, part * LOAD_COLS:(part + 1) * LOAD_COLS])
+        offsets = held.tile([P, LOOKUPS * V // GROUP], U16, name="offsets")
+        nc.sync.dma_start(offsets[:], offs)
+        weights = []
+        for d, u in enumerate((u0, u1)):
+            weights.append(held.tile([P, V], F32, name=f"u{d}_sb"))
+            nc.sync.dma_start(weights[d][:], u)
+
+        tab = held.tile([P, S], F32, name="tab")
+        banks = [psum.tile([P, STRIP], F32, name=f"bank{b}") for b in range(BANKS)]
+        strips_per_load = LOAD_COLS // STRIP
+        for part in range(S // LOAD_COLS):
+            for c in range(passes):
+                for k in range(strips_per_load):
+                    b = part * strips_per_load + k
+                    nc.tensor.matmul(banks[b][:], wt_sb[:, c * P:(c + 1) * P], z_sb[part, c][:, k * STRIP:(k + 1) * STRIP],
+                                     start=(c == 0), stop=(c == passes - 1))
+                    if c == passes - 1:
+                        strip = tab[:, b * STRIP:(b + 1) * STRIP]
+                        if b % 2 == 0:
+                            nc.vector.tensor_copy(strip, banks[b][:])
+                        else:
+                            nc.scalar.copy(strip, banks[b][:])
+
+        width = V // OUT_PIECES
+        for piece in range(OUT_PIECES):
+            cols = slice(piece * width, (piece + 1) * width)
+            products = []
+            for d in range(LOOKUPS):
+                first = (d * V + piece * width) // GROUP
+                products.append(held.tile([P, width], F32, name=f"product_{piece}_{d}"))
+                nc.vector.tensor_tensor(products[d][:], tab[:].indirect(offsets[:, first:first + width // GROUP]),
+                                        weights[d][:, cols], MULT)
+            total = held.tile([P, width], F32, name=f"total_{piece}")
+            nc.vector.tensor_tensor(total[:], products[0][:], products[1][:], ADD)
+            nc.sync.dma_start(out[:, cols], total[:])

@@ -10,6 +10,7 @@ BANKS = 8
 STRIP = S // BANKS
 LOAD_COLS = 1024
 OUT_PIECES = 2
+WARM_MATMULS, WARM_COLS, WARM_ROWS = 2, 256, 32
 FLOPS = 2 * H * P * S
 
 BF16, F32, U16 = mybir.dt.bfloat16, mybir.dt.float32, mybir.dt.uint16
@@ -37,6 +38,12 @@ def tile_lookup_pjmix_out_kernel(tc, z, wt, u0, u1, offs, out):
         for d, u in enumerate((u0, u1)):
             weights.append(held.tile([P, V], F32, name=f"u{d}_sb"))
             nc.sync.dma_start(weights[d][:], u)
+
+        zeros = held.tile([P, WARM_COLS], F32, name="zeros")
+        nc.vector.memset(zeros[:], 0.0)
+        unread = psum.tile([WARM_ROWS, WARM_COLS], F32, name="unread", tag=f"bank{BANKS - 1}")
+        for w in range(WARM_MATMULS):
+            nc.tensor.matmul(unread[:], zeros[:, :WARM_ROWS], zeros[:], start=True, stop=True)
 
         tab = held.tile([P, S], F32, name="tab")
         banks = [psum.tile([P, STRIP], F32, name=f"bank{b}") for b in range(BANKS)]

@@ -8,9 +8,9 @@ LOOKUPS = 2
 GROUP = 16
 BANKS = 8
 STRIP = S // BANKS
-LOAD_COLS = 1024
-OUT_PIECES = 2
-WARM_MATMULS, WARM_COLS, WARM_ROWS = 2, 256, 32
+PART_COLS = (1024, 512, 512)
+PIECE_COLS = (384, 128)
+WARM_MATMULS, WARM_COLS, WARM_ROWS = 3, 128, 32
 FLOPS = 2 * H * P * S
 
 BF16, F32, U16 = mybir.dt.bfloat16, mybir.dt.float32, mybir.dt.uint16
@@ -25,13 +25,14 @@ def tile_lookup_pjmix_out_kernel(tc, z, wt, u0, u1, offs, out):
         tc.psum_pool(name="psum", bufs=1) as psum,
     ):
         wt_sb = held.tile([P, passes * P], BF16, name="wt_sb")
-        nc.sync.dma_start(wt_sb[:], wt.rearrange("(p c) r -> p (c r)", c=passes))
+        nc.scalar.dma_start(wt_sb[:], wt.rearrange("(p c) r -> p (c r)", c=passes))
         z_by_pass = z.rearrange("(p c) s -> c p s", c=passes)
         z_sb = {}
-        for part in range(S // LOAD_COLS):
+        for part, part_cols in enumerate(PART_COLS):
+            part_start = sum(PART_COLS[:part])
             for c in range(passes):
-                z_sb[part, c] = held.tile([P, LOAD_COLS], BF16, name=f"z_{part}_{c}")
-                nc.sync.dma_start(z_sb[part, c][:], z_by_pass[c, :, part * LOAD_COLS:(part + 1) * LOAD_COLS])
+                z_sb[part, c] = held.tile([P, part_cols], BF16, name=f"z_{part}_{c}")
+                nc.sync.dma_start(z_sb[part, c][:], z_by_pass[c, :, part_start:part_start + part_cols])
         offsets = held.tile([P, LOOKUPS * V // GROUP], U16, name="offsets")
         nc.sync.dma_start(offsets[:], offs)
         weights = []
@@ -47,11 +48,11 @@ def tile_lookup_pjmix_out_kernel(tc, z, wt, u0, u1, offs, out):
 
         tab = held.tile([P, S], F32, name="tab")
         banks = [psum.tile([P, STRIP], F32, name=f"bank{b}") for b in range(BANKS)]
-        strips_per_load = LOAD_COLS // STRIP
-        for part in range(S // LOAD_COLS):
+        for part, part_cols in enumerate(PART_COLS):
+            first_strip = sum(PART_COLS[:part]) // STRIP
             for c in range(passes):
-                for k in range(strips_per_load):
-                    b = part * strips_per_load + k
+                for k in range(part_cols // STRIP):
+                    b = first_strip + k
                     nc.tensor.matmul(banks[b][:], wt_sb[:, c * P:(c + 1) * P], z_sb[part, c][:, k * STRIP:(k + 1) * STRIP],
                                      start=(c == 0), stop=(c == passes - 1))
                     if c == passes - 1:
@@ -61,12 +62,12 @@ def tile_lookup_pjmix_out_kernel(tc, z, wt, u0, u1, offs, out):
                         else:
                             nc.scalar.copy(strip, banks[b][:])
 
-        width = V // OUT_PIECES
-        for piece in range(OUT_PIECES):
-            cols = slice(piece * width, (piece + 1) * width)
+        for piece, width in enumerate(PIECE_COLS):
+            piece_start = sum(PIECE_COLS[:piece])
+            cols = slice(piece_start, piece_start + width)
             products = []
             for d in range(LOOKUPS):
-                first = (d * V + piece * width) // GROUP
+                first = (d * V + piece_start) // GROUP
                 products.append(held.tile([P, width], F32, name=f"product_{piece}_{d}"))
                 nc.vector.tensor_tensor(products[d][:], tab[:].indirect(offsets[:, first:first + width // GROUP]),
                                         weights[d][:, cols], MULT)

@@ -9,7 +9,7 @@ GROUP = 16
 BANKS = 8
 STRIP = S // BANKS
 PART_COLS = (1024, 512, 512)
-PIECE_COLS = (384, 128)
+PIECE_COLS = (256, 128, 128)
 WARM_MATMULS, WARM_COLS, WARM_ROWS = 3, 128, 32
 FLOPS = 2 * H * P * S
 
@@ -62,15 +62,25 @@ def tile_lookup_pjmix_out_kernel(tc, z, wt, u0, u1, offs, out):
                         else:
                             nc.scalar.copy(strip, banks[b][:])
 
-        for piece, width in enumerate(PIECE_COLS):
-            piece_start = sum(PIECE_COLS[:piece])
-            cols = slice(piece_start, piece_start + width)
+        def look_up(piece):
+            start, width = sum(PIECE_COLS[:piece]), PIECE_COLS[piece]
             products = []
             for d in range(LOOKUPS):
-                first = (d * V + piece_start) // GROUP
+                first = (d * V + start) // GROUP
                 products.append(held.tile([P, width], F32, name=f"product_{piece}_{d}"))
                 nc.vector.tensor_tensor(products[d][:], tab[:].indirect(offsets[:, first:first + width // GROUP]),
-                                        weights[d][:, cols], MULT)
+                                        weights[d][:, start:start + width], MULT)
+            return products
+
+        def sum_and_store(piece, products):
+            start, width = sum(PIECE_COLS[:piece]), PIECE_COLS[piece]
             total = held.tile([P, width], F32, name=f"total_{piece}")
             nc.vector.tensor_tensor(total[:], products[0][:], products[1][:], ADD)
-            nc.sync.dma_start(out[:, cols], total[:])
+            nc.sync.dma_start(out[:, start:start + width], total[:])
+
+        pending = look_up(0)
+        for piece in range(1, len(PIECE_COLS)):
+            following = look_up(piece)
+            sum_and_store(piece - 1, pending)
+            pending = following
+        sum_and_store(len(PIECE_COLS) - 1, pending)

import concourse.mybir as mybir

P = 128
H = 256
S = 2048
V = 512
LOOKUPS = 2
GROUP = 16
BANKS = 8
STRIP = S // BANKS
PART_COLS = (1024, 512, 512)
PIECE_COLS = (256, 128, 128)
WARM_MATMULS, WARM_COLS, WARM_ROWS = 3, 128, 32
FLOPS = 2 * H * P * S

BF16, F32, U16 = mybir.dt.bfloat16, mybir.dt.float32, mybir.dt.uint16
MULT, ADD = mybir.AluOpType.mult, mybir.AluOpType.add


def tile_lookup_pjmix_out_kernel(tc, z, wt, u0, u1, offs, out):
    nc = tc.nc
    passes = H // P
    with (
        tc.tile_pool(name="held", bufs=1) as held,
        tc.psum_pool(name="psum", bufs=1) as psum,
    ):
        wt_sb = held.tile([P, passes * P], BF16, name="wt_sb")
        nc.scalar.dma_start(wt_sb[:], wt.rearrange("(p c) r -> p (c r)", c=passes))
        z_by_pass = z.rearrange("(p c) s -> c p s", c=passes)
        z_sb = {}
        for part, part_cols in enumerate(PART_COLS):
            part_start = sum(PART_COLS[:part])
            for c in range(passes):
                z_sb[part, c] = held.tile([P, part_cols], BF16, name=f"z_{part}_{c}")
                nc.sync.dma_start(z_sb[part, c][:], z_by_pass[c, :, part_start:part_start + part_cols])
        offsets = held.tile([P, LOOKUPS * V // GROUP], U16, name="offsets")
        nc.sync.dma_start(offsets[:], offs)
        weights = []
        for d, u in enumerate((u0, u1)):
            weights.append(held.tile([P, V], F32, name=f"u{d}_sb"))
            nc.sync.dma_start(weights[d][:], u)

        zeros = held.tile([P, WARM_COLS], F32, name="zeros")
        nc.vector.memset(zeros[:], 0.0)
        unread = psum.tile([WARM_ROWS, WARM_COLS], F32, name="unread", tag=f"bank{BANKS - 1}")
        for w in range(WARM_MATMULS):
            nc.tensor.matmul(unread[:], zeros[:, :WARM_ROWS], zeros[:], start=True, stop=True)

        tab = held.tile([P, S], F32, name="tab")
        banks = [psum.tile([P, STRIP], F32, name=f"bank{b}") for b in range(BANKS)]
        for part, part_cols in enumerate(PART_COLS):
            first_strip = sum(PART_COLS[:part]) // STRIP
            for c in range(passes):
                for k in range(part_cols // STRIP):
                    b = first_strip + k
                    nc.tensor.matmul(banks[b][:], wt_sb[:, c * P:(c + 1) * P], z_sb[part, c][:, k * STRIP:(k + 1) * STRIP],
                                     start=(c == 0), stop=(c == passes - 1))
                    if c == passes - 1:
                        strip = tab[:, b * STRIP:(b + 1) * STRIP]
                        if b % 2 == 0:
                            nc.vector.tensor_copy(strip, banks[b][:])
                        else:
                            nc.scalar.copy(strip, banks[b][:])

        def look_up(piece):
            start, width = sum(PIECE_COLS[:piece]), PIECE_COLS[piece]
            products = []
            for d in range(LOOKUPS):
                first = (d * V + start) // GROUP
                products.append(held.tile([P, width], F32, name=f"product_{piece}_{d}"))
                nc.vector.tensor_tensor(products[d][:], tab[:].indirect(offsets[:, first:first + width // GROUP]),
                                        weights[d][:, start:start + width], MULT)
            return products

        def sum_and_store(piece, products):
            start, width = sum(PIECE_COLS[:piece]), PIECE_COLS[piece]
            total = held.tile([P, width], F32, name=f"total_{piece}")
            nc.vector.tensor_tensor(total[:], products[0][:], products[1][:], ADD)
            nc.sync.dma_start(out[:, start:start + width], total[:])

        pending = look_up(0)
        for piece in range(1, len(PIECE_COLS)):
            following = look_up(piece)
            sum_and_store(piece - 1, pending)
            pending = following
        sum_and_store(len(PIECE_COLS) - 1, pending)
